import numpy as np
import ml_dtypes


def mxq(x, axis, fmt="e4m3"):
    dtype, down = {"e4m3": (ml_dtypes.float8_e4m3fn, 7), "e5m2": (ml_dtypes.float8_e5m2, 14)}[fmt]
    v = np.moveaxis(np.asarray(x, np.float32).astype(ml_dtypes.bfloat16).astype(np.float64), axis, -1)
    blocks = v.reshape(v.shape[:-1] + (-1, 32))
    amax = np.abs(blocks).max(-1, keepdims=True)
    byte = np.maximum(np.where(amax > 0, np.frexp(amax)[1] - 1 + 127, 0) - down, 1)
    scale = np.exp2(byte - 127.0)
    codes = (blocks / scale).astype(np.float32).astype(dtype).astype(np.float64)
    return np.moveaxis((codes * scale).reshape(v.shape), -1, axis)


WIDE = False


def mx_kscale(k, group=512):
    if not WIDE:
        return np.ones(k)
    levels = np.array([18, -18])
    if group != 512:
        return np.exp2(np.random.permutation(np.resize(levels, k // group))).repeat(group)
    if k % 512:
        return np.exp2(np.random.permutation(np.resize(levels, k // 32))).repeat(32)
    a = np.empty((k // 512, 16))
    for p in range(k // 512):
        a[p, :8] = np.random.permutation(np.resize(levels, 8))
        for g in range(8):
            far = levels[np.abs(levels - a[p, g]) >= 10]
            a[p, g + 8] = far[np.random.randint(len(far))]
    return np.exp2(a.ravel()).repeat(32)


def f64(x):
    return np.asarray(x).astype(np.float64)


E2M1 = np.array([0.0, 0.5, 1.0, 1.5, 2.0, 3.0, 4.0, 6.0, -0.0, -0.5, -1.0, -1.5, -2.0, -3.0, -4.0, -6.0])


def pack_group(w):
    k, n = w.shape
    w = f64(np.asarray(w, np.float32).astype(ml_dtypes.bfloat16)).reshape(k // 32, 32, n)
    amax = np.abs(w).max(1)
    mant, ex = np.frexp(amax / 6.0)
    byte = np.clip(np.where(amax > 0, np.where(mant > 0.5, ex, ex - 1) + 127, 1), 1, 254)
    scaled = (w * np.exp2(127.0 - byte)[:, None, :]).reshape(k, n).astype(np.float32)
    c = np.ascontiguousarray(scaled.reshape(k // 4, 4, n).transpose(0, 2, 1)).astype(ml_dtypes.float4_e2m1fn).view(np.uint8) & 0xF
    return np.ascontiguousarray((c[..., 0::2] | (c[..., 1::2] << 4)).reshape(k // 4, 2 * n)), byte.astype(np.uint8)


def unpack_group(words, scales):
    p, n = words.shape[0], scales.shape[1]
    words = np.ascontiguousarray(words).reshape(p, n, 2)
    nib = np.empty((p, n, 4), np.uint8)
    nib[..., 0::2] = words & 0xF
    nib[..., 1::2] = words >> 4
    return E2M1[nib].transpose(0, 2, 1).reshape(4 * p, n) * np.repeat(np.exp2(scales.astype(np.float64) - 127.0), 32, axis=0)


G, D, M, N = 4, 128, 256, 1024


def setup_inputs():
    n = np.random.standard_normal
    s = mx_kscale(D, 0)[:, None]
    w_ = [pack_group(w) for w in n((G, D, M)) / np.sqrt(D) / s]
    return {
        "x": (n((G, D, N)) * s).astype(np.float32),
        "w_words": np.stack([w[0] for w in w_]),
        "w_scales": np.stack([w[1] for w in w_]),
        "r": n((G, M, N)).astype(np.float32),
    }


def reference(x, w_words, w_scales, r):
    xq = mxq(f64(x), 1, "e4m3")
    y = np.stack([unpack_group(w_words[g], w_scales[g]) for g in range(G)]).transpose(0, 2, 1) @ xq
    y = 1.0 / (1.0 + np.exp(-(y)))
    y = y + f64(r)
    return y

@@ -1,0 +1,123 @@
+from contextlib import ExitStack
+
+import concourse.mybir as mybir
+
+G, D, M, N = 4, 128, 256, 1024
+FLOPS = 2 * G * D * M * N
+
+F32 = mybir.dt.float32
+BF16 = mybir.dt.bfloat16
+I32 = mybir.dt.int32
+U32 = mybir.dt.uint32
+U8 = mybir.dt.uint8
+FP8X4 = mybir.dt.float8_e4m3fn_x4
+FP4X4 = mybir.dt.float4_e2m1fn_x4
+
+P = 128
+PACK = 4
+ROWS = D // PACK
+BLOCKS = D // 32
+PAIR = M // P
+N_TILE = 512
+HALVES = N // N_TILE
+RUN = 4
+
+
+def tile_rows_glin_sigmoid_res_kernel(tc, x, w_words, w_scales, r, out):
+    nc = tc.nc
+    with ExitStack() as ctx:
+        sb = ctx.enter_context(tc.tile_pool(name="sb", bufs=1))
+        psum = ctx.enter_context(tc.psum_pool(name="psum", bufs=1))
+        ctx.enter_context(tc.manual_schedule())
+
+        x_raw = sb.tile([P, PACK * N], F32, name="x_raw", align_bytes=64)
+        nc.sync.dma_start(out=x_raw[:], in_=x.rearrange("g (p j) n -> (g p) (j n)", j=PACK))
+
+        words_raw = sb.tile([P, 2 * M], U8, name="words_raw", align_bytes=64)
+        scales_raw = sb.tile([P, M], U8, name="scales_raw", align_bytes=64)
+        nc.vector.memset(scales_raw[:].bitcast(I32), 0)
+        nc.scalar.dma_start(
+            out=words_raw[:].bitcast(I32),
+            in_=w_words.rearrange("g p b -> (g p) b").bitcast(I32),
+        )
+        for g in range(G):
+            nc.scalar.dma_start(
+                out=scales_raw[ROWS * g : ROWS * g + BLOCKS, :].bitcast(I32),
+                in_=w_scales[g].bitcast(I32),
+            )
+
+        res = []
+        for g in range(G):
+            res_g = sb.tile([P, PAIR * N], F32, name="res%d" % g, align_bytes=64)
+            nc.sync.dma_start(out=res_g[:], in_=r[g].rearrange("(q h) n -> q (h n)", h=PAIR))
+            res.append(res_g)
+
+        words = sb.tile([P, 2 * M], U8, name="words", align_bytes=64)
+        scales = sb.tile([P, M], U8, name="scales", align_bytes=64)
+        nc.vector.tensor_copy(
+            out=words[:].rearrange("p (h q b) -> p q h b", h=PAIR, b=2),
+            in_=words_raw[:].rearrange("p (q h b) -> p q h b", h=PAIR, b=2),
+        )
+        nc.vector.tensor_copy(
+            out=scales[:].rearrange("p (h q) -> p q h", h=PAIR),
+            in_=scales_raw[:].rearrange("p (q h) -> p q h", h=PAIR),
+        )
+
+        codes, x_scales = [], []
+        x_view = x_raw[:].rearrange("p (j c i) -> p c j i", j=PACK, i=RUN)
+        runs = N_TILE // RUN
+        for t in range(HALVES):
+            x_bf = sb.tile([P, N_TILE * PACK], BF16, name="x_bf%d" % t, align_bytes=64)
+            codes_t = sb.tile([P, N_TILE], U32, name="codes%d" % t, align_bytes=64)
+            x_scales_t = sb.tile([P, N_TILE], U8, name="x_scales%d" % t, align_bytes=64)
+            nc.vector.tensor_copy(
+                out=x_bf[:].rearrange("p (c i j) -> p c j i", i=RUN, j=PACK),
+                in_=x_view[:, t * runs : (t + 1) * runs, :, :],
+            )
+            nc.vector.quantize_mx(out=codes_t[:].bitcast(FP8X4), scales=x_scales_t[:], in_=x_bf[:])
+            codes.append(codes_t)
+            x_scales.append(x_scales_t)
+
+        banks = {}
+        for g in range(G):
+            for h in range(PAIR):
+                banks[g, h] = psum.tile([P, N_TILE], F32, name="bank%d_%d" % (g, h))
+
+        def multiply(g, h, t):
+            rows = slice(ROWS * g, ROWS * (g + 1))
+            nc.tensor.matmul_mx(
+                out=banks[g, h][:],
+                lhsT=words[rows, 2 * P * h : 2 * P * (h + 1)].bitcast(FP4X4),
+                lhsT_scale=scales[rows, P * h : P * (h + 1)],
+                rhs=codes[t][rows, :].bitcast(FP8X4),
+                rhs_scale=x_scales[t][rows, :],
+                start=True,
+                stop=True,
+            )
+
+        for g in range(G):
+            for h in range(PAIR):
+                multiply(g, h, 0)
+
+        y = []
+        for g in range(G):
+            y.append(sb.tile([P, PAIR * N], F32, name="y%d" % g, align_bytes=64))
+
+        order = [(g, h, t) for g in range(G) for t in range(HALVES) for h in range(PAIR)]
+        for g in range(1, G):
+            first = order.index((g, 0, 0))
+            order.remove((g, 0, 0))
+            order = order[: first - 2] + [(g, 0, 0)] + order[first - 2 :]
+
+        for g, h, t in order:
+            cols = slice(h * N + t * N_TILE, h * N + (t + 1) * N_TILE)
+            nc.scalar.activation(
+                out=y[g][:, cols], in_=banks[g, h][:], func=mybir.ActivationFunctionType.Sigmoid
+            )
+            if t + 1 < HALVES:
+                multiply(g, h, t + 1)
+            nc.vector.tensor_tensor(
+                out=y[g][:, cols], in0=y[g][:, cols], in1=res[g][:, cols], op=mybir.AluOpType.add
+            )
+            if (h, t) == (PAIR - 1, HALVES - 1):
+                nc.sync.dma_start(out=out[g].rearrange("(q h) n -> q (h n)", h=PAIR), in_=y[g][:])

@@ -21,6 +21,7 @@ PAIR = M // P
 N_TILE = 512
 HALVES = N // N_TILE
 RUN = 4
+VECTOR_COLS = (344, 208)
 
 
 def tile_rows_glin_sigmoid_res_kernel(tc, x, w_words, w_scales, r, out):
@@ -46,6 +47,11 @@ def tile_rows_glin_sigmoid_res_kernel(tc, x, w_words, w_scales, r, out):
                 in_=w_scales[g].bitcast(I32),
             )
 
+        warm_in = sb.tile([P, 1], F32, name="warm_in")
+        warm_out = sb.tile([P, 1], F32, name="warm_out")
+        nc.vector.memset(warm_in[:], 0.0)
+        nc.scalar.activation(out=warm_out[:], in_=warm_in[:], func=mybir.ActivationFunctionType.Sigmoid)
+
         res = []
         for g in range(G):
             res_g = sb.tile([P, PAIR * N], F32, name="res%d" % g, align_bytes=64)
@@ -70,9 +76,13 @@ def tile_rows_glin_sigmoid_res_kernel(tc, x, w_words, w_scales, r, out):
             x_bf = sb.tile([P, N_TILE * PACK], BF16, name="x_bf%d" % t, align_bytes=64)
             codes_t = sb.tile([P, N_TILE], U32, name="codes%d" % t, align_bytes=64)
             x_scales_t = sb.tile([P, N_TILE], U8, name="x_scales%d" % t, align_bytes=64)
+            bf_view = x_bf[:].rearrange("p (c i j) -> p c j i", i=RUN, j=PACK)
+            cut = VECTOR_COLS[t] // RUN
             nc.vector.tensor_copy(
-                out=x_bf[:].rearrange("p (c i j) -> p c j i", i=RUN, j=PACK),
-                in_=x_view[:, t * runs : (t + 1) * runs, :, :],
+                out=bf_view[:, :cut, :, :], in_=x_view[:, t * runs : t * runs + cut, :, :]
+            )
+            nc.scalar.copy(
+                out=bf_view[:, cut:, :, :], in_=x_view[:, t * runs + cut : (t + 1) * runs, :, :]
             )
             nc.vector.quantize_mx(out=codes_t[:].bitcast(FP8X4), scales=x_scales_t[:], in_=x_bf[:])
             codes.append(codes_t)

@@ -22,6 +22,7 @@ N_TILE = 512
 HALVES = N // N_TILE
 RUN = 4
 VECTOR_COLS = (344, 208)
+FIRST_LEAD = 3
 
 
 def tile_rows_glin_sigmoid_res_kernel(tc, x, w_words, w_scales, r, out):
@@ -42,7 +43,7 @@ def tile_rows_glin_sigmoid_res_kernel(tc, x, w_words, w_scales, r, out):
             in_=w_words.rearrange("g p b -> (g p) b").bitcast(I32),
         )
         for g in range(G):
-            nc.scalar.dma_start(
+            nc.sync.dma_start(
                 out=scales_raw[ROWS * g : ROWS * g + BLOCKS, :].bitcast(I32),
                 in_=w_scales[g].bitcast(I32),
             )
@@ -64,10 +65,6 @@ def tile_rows_glin_sigmoid_res_kernel(tc, x, w_words, w_scales, r, out):
             out=words[:].rearrange("p (h q b) -> p q h b", h=PAIR, b=2),
             in_=words_raw[:].rearrange("p (q h b) -> p q h b", h=PAIR, b=2),
         )
-        nc.vector.tensor_copy(
-            out=scales[:].rearrange("p (h q) -> p q h", h=PAIR),
-            in_=scales_raw[:].rearrange("p (q h) -> p q h", h=PAIR),
-        )
 
         codes, x_scales = [], []
         x_view = x_raw[:].rearrange("p (j c i) -> p c j i", j=PACK, i=RUN)
@@ -84,6 +81,11 @@ def tile_rows_glin_sigmoid_res_kernel(tc, x, w_words, w_scales, r, out):
             nc.scalar.copy(
                 out=bf_view[:, cut:, :, :], in_=x_view[:, t * runs + cut : (t + 1) * runs, :, :]
             )
+            if t == 0:
+                nc.vector.tensor_copy(
+                    out=scales[:].rearrange("p (h q) -> p q h", h=PAIR),
+                    in_=scales_raw[:].rearrange("p (q h) -> p q h", h=PAIR),
+                )
             nc.vector.quantize_mx(out=codes_t[:].bitcast(FP8X4), scales=x_scales_t[:], in_=x_bf[:])
             codes.append(codes_t)
             x_scales.append(x_scales_t)
@@ -105,27 +107,25 @@ def tile_rows_glin_sigmoid_res_kernel(tc, x, w_words, w_scales, r, out):
                 stop=True,
             )
 
-        for g in range(G):
-            for h in range(PAIR):
-                multiply(g, h, 0)
-
         y = []
         for g in range(G):
             y.append(sb.tile([P, PAIR * N], F32, name="y%d" % g, align_bytes=64))
 
-        order = [(g, h, t) for g in range(G) for t in range(HALVES) for h in range(PAIR)]
-        for g in range(1, G):
-            first = order.index((g, 0, 0))
-            order.remove((g, 0, 0))
-            order = order[: first - 2] + [(g, 0, 0)] + order[first - 2 :]
+        first_halves = [(g, h, 0) for g in range(G) for h in range(PAIR)]
+        order = first_halves[:FIRST_LEAD]
+        taken = FIRST_LEAD
+        for g in range(G):
+            order = order + [(g, h, 1) for h in range(PAIR)]
+            upto = PAIR * (g + 3)
+            order = order + first_halves[taken:upto]
+            taken = upto
 
         for g, h, t in order:
             cols = slice(h * N + t * N_TILE, h * N + (t + 1) * N_TILE)
+            multiply(g, h, t)
             nc.scalar.activation(
                 out=y[g][:, cols], in_=banks[g, h][:], func=mybir.ActivationFunctionType.Sigmoid
             )
-            if t + 1 < HALVES:
-                multiply(g, h, t + 1)
             nc.vector.tensor_tensor(
                 out=y[g][:, cols], in0=y[g][:, cols], in1=res[g][:, cols], op=mybir.AluOpType.add
             )

from contextlib import ExitStack

import concourse.mybir as mybir

G, D, M, N = 4, 128, 256, 1024
FLOPS = 2 * G * D * M * N

F32 = mybir.dt.float32
BF16 = mybir.dt.bfloat16
I32 = mybir.dt.int32
U32 = mybir.dt.uint32
U8 = mybir.dt.uint8
FP8X4 = mybir.dt.float8_e4m3fn_x4
FP4X4 = mybir.dt.float4_e2m1fn_x4

P = 128
PACK = 4
ROWS = D // PACK
BLOCKS = D // 32
PAIR = M // P
N_TILE = 512
HALVES = N // N_TILE
RUN = 4
VECTOR_COLS = (344, 208)
FIRST_LEAD = 3


def tile_rows_glin_sigmoid_res_kernel(tc, x, w_words, w_scales, r, out):
    nc = tc.nc
    with ExitStack() as ctx:
        sb = ctx.enter_context(tc.tile_pool(name="sb", bufs=1))
        psum = ctx.enter_context(tc.psum_pool(name="psum", bufs=1))
        ctx.enter_context(tc.manual_schedule())

        x_raw = sb.tile([P, PACK * N], F32, name="x_raw", align_bytes=64)
        nc.sync.dma_start(out=x_raw[:], in_=x.rearrange("g (p j) n -> (g p) (j n)", j=PACK))

        words_raw = sb.tile([P, 2 * M], U8, name="words_raw", align_bytes=64)
        scales_raw = sb.tile([P, M], U8, name="scales_raw", align_bytes=64)
        nc.vector.memset(scales_raw[:].bitcast(I32), 0)
        nc.scalar.dma_start(
            out=words_raw[:].bitcast(I32),
            in_=w_words.rearrange("g p b -> (g p) b").bitcast(I32),
        )
        for g in range(G):
            nc.sync.dma_start(
                out=scales_raw[ROWS * g : ROWS * g + BLOCKS, :].bitcast(I32),
                in_=w_scales[g].bitcast(I32),
            )

        warm_in = sb.tile([P, 1], F32, name="warm_in")
        warm_out = sb.tile([P, 1], F32, name="warm_out")
        nc.vector.memset(warm_in[:], 0.0)
        nc.scalar.activation(out=warm_out[:], in_=warm_in[:], func=mybir.ActivationFunctionType.Sigmoid)

        res = []
        for g in range(G):
            res_g = sb.tile([P, PAIR * N], F32, name="res%d" % g, align_bytes=64)
            nc.sync.dma_start(out=res_g[:], in_=r[g].rearrange("(q h) n -> q (h n)", h=PAIR))
            res.append(res_g)

        words = sb.tile([P, 2 * M], U8, name="words", align_bytes=64)
        scales = sb.tile([P, M], U8, name="scales", align_bytes=64)
        nc.vector.tensor_copy(
            out=words[:].rearrange("p (h q b) -> p q h b", h=PAIR, b=2),
            in_=words_raw[:].rearrange("p (q h b) -> p q h b", h=PAIR, b=2),
        )

        codes, x_scales = [], []
        x_view = x_raw[:].rearrange("p (j c i) -> p c j i", j=PACK, i=RUN)
        runs = N_TILE // RUN
        for t in range(HALVES):
            x_bf = sb.tile([P, N_TILE * PACK], BF16, name="x_bf%d" % t, align_bytes=64)
            codes_t = sb.tile([P, N_TILE], U32, name="codes%d" % t, align_bytes=64)
            x_scales_t = sb.tile([P, N_TILE], U8, name="x_scales%d" % t, align_bytes=64)
            bf_view = x_bf[:].rearrange("p (c i j) -> p c j i", i=RUN, j=PACK)
            cut = VECTOR_COLS[t] // RUN
            nc.vector.tensor_copy(
                out=bf_view[:, :cut, :, :], in_=x_view[:, t * runs : t * runs + cut, :, :]
            )
            nc.scalar.copy(
                out=bf_view[:, cut:, :, :], in_=x_view[:, t * runs + cut : (t + 1) * runs, :, :]
            )
            if t == 0:
                nc.vector.tensor_copy(
                    out=scales[:].rearrange("p (h q) -> p q h", h=PAIR),
                    in_=scales_raw[:].rearrange("p (q h) -> p q h", h=PAIR),
                )
            nc.vector.quantize_mx(out=codes_t[:].bitcast(FP8X4), scales=x_scales_t[:], in_=x_bf[:])
            codes.append(codes_t)
            x_scales.append(x_scales_t)

        banks = {}
        for g in range(G):
            for h in range(PAIR):
                banks[g, h] = psum.tile([P, N_TILE], F32, name="bank%d_%d" % (g, h))

        def multiply(g, h, t):
            rows = slice(ROWS * g, ROWS * (g + 1))
            nc.tensor.matmul_mx(
                out=banks[g, h][:],
                lhsT=words[rows, 2 * P * h : 2 * P * (h + 1)].bitcast(FP4X4),
                lhsT_scale=scales[rows, P * h : P * (h + 1)],
                rhs=codes[t][rows, :].bitcast(FP8X4),
                rhs_scale=x_scales[t][rows, :],
                start=True,
                stop=True,
            )

        y = []
        for g in range(G):
            y.append(sb.tile([P, PAIR * N], F32, name="y%d" % g, align_bytes=64))

        first_halves = [(g, h, 0) for g in range(G) for h in range(PAIR)]
        order = first_halves[:FIRST_LEAD]
        taken = FIRST_LEAD
        for g in range(G):
            order = order + [(g, h, 1) for h in range(PAIR)]
            upto = PAIR * (g + 3)
            order = order + first_halves[taken:upto]
            taken = upto

        for g, h, t in order:
            cols = slice(h * N + t * N_TILE, h * N + (t + 1) * N_TILE)
            multiply(g, h, t)
            nc.scalar.activation(
                out=y[g][:, cols], in_=banks[g, h][:], func=mybir.ActivationFunctionType.Sigmoid
            )
            nc.vector.tensor_tensor(
                out=y[g][:, cols], in0=y[g][:, cols], in1=res[g][:, cols], op=mybir.AluOpType.add
            )
            if (h, t) == (PAIR - 1, HALVES - 1):
                nc.sync.dma_start(out=out[g].rearrange("(q h) n -> q (h n)", h=PAIR), in_=y[g][:])
